import numpy as np
import ml_dtypes


def mxq(x, axis, fmt="e4m3"):
    dtype, down = {"e4m3": (ml_dtypes.float8_e4m3fn, 7), "e5m2": (ml_dtypes.float8_e5m2, 14)}[fmt]
    v = np.moveaxis(np.asarray(x, np.float32).astype(ml_dtypes.bfloat16).astype(np.float64), axis, -1)
    blocks = v.reshape(v.shape[:-1] + (-1, 32))
    amax = np.abs(blocks).max(-1, keepdims=True)
    byte = np.maximum(np.where(amax > 0, np.frexp(amax)[1] - 1 + 127, 0) - down, 1)
    scale = np.exp2(byte - 127.0)
    codes = (blocks / scale).astype(np.float32).astype(dtype).astype(np.float64)
    return np.moveaxis((codes * scale).reshape(v.shape), -1, axis)


WIDE = False


def mx_kscale(k):
    if not WIDE:
        return np.ones(k)
    levels = np.array([10, -10, 5, -5, 0])
    if k % 512:
        return np.exp2(np.random.permutation(np.resize(levels, k // 32))).repeat(32)
    a = np.empty((k // 512, 16))
    for p in range(k // 512):
        a[p, :8] = np.random.permutation(np.resize(levels, 8))
        for g in range(8):
            far = levels[np.abs(levels - a[p, g]) >= 10]
            a[p, g + 8] = far[np.random.randint(len(far))]
    return np.exp2(a.ravel()).repeat(32)


def f64(x):
    return np.asarray(x).astype(np.float64)


def striped(idx):
    return np.tile(idx.reshape(-1, 16).T, (8, 1)).astype(np.uint16)


def unstriped(offs):
    return offs[:16].T.reshape(-1).astype(np.int64)


E2M1 = np.array([0.0, 0.5, 1.0, 1.5, 2.0, 3.0, 4.0, 6.0, -0.0, -0.5, -1.0, -1.5, -2.0, -3.0, -4.0, -6.0])


def pack_weight(w, fmt):
    k, n = w.shape
    w = f64(np.asarray(w, np.float32).astype(ml_dtypes.bfloat16)).reshape(k // 32, 32, n)
    amax = np.abs(w).max(1)
    if fmt == "e4m3":
        byte = np.frexp(amax)[1] - 1 + 127 - 7
    else:
        mant, ex = np.frexp(amax / 6.0)
        byte = np.where(mant > 0.5, ex, ex - 1) + 127
    byte = np.clip(np.where(amax > 0, byte, 1), 1, 254)
    scaled = (w * np.exp2(127.0 - byte)[:, None, :]).reshape(k, n).astype(np.float32)
    by_word = np.ascontiguousarray(scaled.reshape(k // 512, 128, 4, n).transpose(0, 1, 3, 2))
    if fmt == "e4m3":
        words = by_word.astype(ml_dtypes.float8_e4m3fn).view(np.uint8)
    else:
        c = by_word.astype(ml_dtypes.float4_e2m1fn).view(np.uint8) & 0xF
        words = (c[..., 0::2] | (c[..., 1::2] << 4)).reshape(k // 512, 128, 2 * n)
    return np.ascontiguousarray(words), np.ascontiguousarray(byte.astype(np.uint8).reshape(k // 512, 16, n))


def unpack_weight(words, scales, fmt):
    g, _, n = scales.shape
    words = np.ascontiguousarray(words).reshape(g, 128, n, -1)
    if fmt == "e4m3":
        vals = words.view(ml_dtypes.float8_e4m3fn).astype(np.float64)
    else:
        nib = np.empty((g, 128, n, 4), np.uint8)
        nib[..., 0::2] = words & 0xF
        nib[..., 1::2] = words >> 4
        vals = E2M1[nib]
    vals = vals * np.repeat(np.exp2(scales.astype(np.float64) - 127.0), 8, axis=1)[..., None]
    return vals.transpose(0, 1, 3, 2).reshape(g * 512, n)


def gelu(v):
    return 0.5 * v * (1.0 + np.tanh(np.sqrt(2.0 / np.pi) * (v + 0.044715 * v**3)))


K, K2, T, T3, S, P, H, N = 1024, 1536, 4096, 2048, 1024, 512, 512, 768

def setup_inputs():
    n = np.random.standard_normal
    s = mx_kscale(K)[:, None]
    s2 = mx_kscale(K2)[:, None]
    u = mx_kscale(H)[:, None]
    d = {}
    d["tab_words"], d["tab_scales"] = pack_weight(n((K, T)) * s, "e4m3")
    d["tab2_words"], d["tab2_scales"] = pack_weight(n((K2, T3)) * s2, "e4m3")
    d["offs"] = striped(np.random.permutation(T)[:S])
    d["offs2"] = striped(np.random.permutation(T3)[:P])
    d["pos1"] = striped(np.random.permutation(S)[:P])
    d["wa"] = (1.2 * n((K, H)) / s * u.T / K ** 0.5).astype(np.float32)
    d["wb_words"], d["wb_scales"] = pack_weight(0.9 * n((K, H)) / s * np.sqrt(u.T) / K ** 0.5, "e2m1")
    d["wc_words"], d["wc_scales"] = pack_weight(n((K2, H)) / s2 / K2 ** 0.5, "e4m3")
    d["gain"] = (2.2 * np.exp(0.3 * n(H))).astype(np.float32)
    d["wgs"] = np.exp(0.3 * n((128, P))).astype(np.float32)
    d["w3"] = (2.0 * n((H, N)) / u / H ** 0.5).astype(np.float32)
    d["w4_words"], d["w4_scales"] = pack_weight(0.7 * n((H, N)) / u / H ** 0.5, "e2m1")
    return d

def reference(tab_words, tab_scales, tab2_words, tab2_scales, offs, offs2, pos1, wa, wb_words, wb_scales, wc_words, wc_scales, gain, wgs, w3, w4_words, w4_scales):
    v = unpack_weight(tab_words, tab_scales, "e4m3")[:, unstriped(offs)]
    v2 = unpack_weight(tab2_words, tab2_scales, "e4m3")[:, unstriped(offs2)]
    lin = mxq(f64(wa), 0, "e4m3").T @ v
    dev = unpack_weight(wb_words, wb_scales, "e2m1").T @ v
    a = lin - np.square(dev)
    b = (unpack_weight(wc_words, wc_scales, "e4m3").T @ v2) * f64(gain)[:, None]
    placed = np.zeros((H, S))
    placed[:, unstriped(pos1)] = np.tile(f64(wgs), (H // 128, 1)) * b
    z = a * (1.0 / (1.0 + np.exp(-placed)))
    yz = mxq(f64(w3), 0, "e4m3").T @ mxq(z, 0, "e4m3")
    ya = unpack_weight(w4_words, w4_scales, "e2m1").T @ mxq(a, 0, "e4m3")
    return yz - ya

@@ -1,0 +1,289 @@
+from contextlib import ExitStack
+
+import concourse.mybir as mybir
+from concourse.masks import make_identity
+
+K, K2, T, T3, S, NG, H, N = 1024, 1536, 4096, 2048, 1024, 512, 512, 768
+FLOPS = 2 * (2 * K * H * S + K2 * H * NG + 2 * H * N * S)
+
+F32 = mybir.dt.float32
+BF16 = mybir.dt.bfloat16
+I32 = mybir.dt.int32
+U32 = mybir.dt.uint32
+U16 = mybir.dt.uint16
+U8 = mybir.dt.uint8
+FP8X4 = mybir.dt.float8_e4m3fn_x4
+FP4X4 = mybir.dt.float4_e2m1fn_x4
+ALU = mybir.AluOpType
+ACT = mybir.ActivationFunctionType
+
+P = 128
+PACK = 4
+HALF = 512
+CHUNK = 256
+
+
+def tile_list_kick_warning_features_kernel(
+    tc, tab_words, tab_scales, tab2_words, tab2_scales, offs, offs2, pos1, wa, wb_words, wb_scales,
+    wc_words, wc_scales, gain, wgs, w3, w4_words, w4_scales, out,
+):
+    nc = tc.nc
+    pa, pb = K // 512, K2 // 512
+
+    with ExitStack() as ctx:
+        lists = ctx.enter_context(tc.tile_pool(name="lists", bufs=1))
+        keep = ctx.enter_context(tc.tile_pool(name="keep", bufs=1))
+        psum = ctx.enter_context(tc.psum_pool(name="psum", bufs=8))
+
+        def held(shape, dtype, name):
+            return keep.tile(shape, dtype, name=name, align_bytes=64)
+
+        def ring(shape, dtype, name, tag, bufs):
+            return keep.tile(shape, dtype, name=name, tag=tag, bufs=bufs, align_bytes=64)
+
+        def bank(name):
+            return psum.tile([P, 512], F32, name=name, tag="bank")
+
+        idx = lists.tile([P, S // 16], U16, name="idx")
+        idx2 = lists.tile([P, NG // 16], U16, name="idx2")
+        places = lists.tile([P, NG // 16], U16, name="places")
+
+        tab2_sc = held([P, T3], U8, "tab2_sc")
+        tab_sc = held([P, T], U8, "tab_sc")
+        wc_sc_raw = held([P, H], U8, "wc_sc_raw")
+        wb_sc_raw = held([P, pa * H], U8, "wb_sc_raw")
+        w4_sc = held([P, N], U8, "w4_sc")
+        v_sc1 = [held([P, HALF], U8, "v_sc1_%d" % h) for h in range(2)]
+        for tile in (tab2_sc, wc_sc_raw, tab_sc, wb_sc_raw, w4_sc, v_sc1[0], v_sc1[1]):
+            nc.vector.memset(tile[:].bitcast(I32), 0)
+
+        def words(dram):
+            return dram.rearrange("p c i -> p (c i)").bitcast(I32)
+
+        tab2_w = [ring([P, T3], I32, "tab2_w%d" % a, tag, 1) for a, tag in enumerate(("a0", "a1", "late"))]
+        tab_w = ring([P, pa * T], I32, "tab_w", "tab_w3", 1)
+        wc_raw = held([P, pb, H], I32, "wc_raw")
+        gain_sb = held([P, PACK], F32, "gain_sb")
+        wgs_sb = held([P, NG], F32, "wgs_sb")
+        ident = held([P, P], F32, "ident")
+        make_identity(nc, ident[:])
+        wb_raw = held([P, pa, H // 2], I32, "wb_raw")
+        wa_raw = ring([P, pa * PACK * H], F32, "wa_raw", "wa_sig", 1)
+        w3_raw = held([P, PACK, N], F32, "w3_raw")
+        w4_w = held([P, N // 2], I32, "w4_w")
+
+        def load_planes(queue, tile, scales, passes):
+            for q in range(4):
+                queue.dma_start(out=tile[32 * q : 32 * q + 4 * passes, :].bitcast(I32),
+                                in_=scales[:, 4 * q : 4 * q + 4, :].bitcast(I32))
+
+        nc.sync.dma_start(idx2[:], offs2)
+        nc.sync.dma_start(out=tab2_w[0][:], in_=words(tab2_words[0]))
+        nc.scalar.dma_start(out=wgs_sb[:], in_=wgs)
+        load_planes(nc.gpsimd, tab2_sc, tab2_scales, pb)
+        load_planes(nc.scalar, wc_sc_raw, wc_scales, pb)
+        load_planes(nc.gpsimd, tab_sc, tab_scales, pa)
+        for q in range(4):
+            nc.scalar.dma_start(out=wb_sc_raw[32 * q : 32 * q + 4, :].bitcast(I32).rearrange("r (a c) -> r a c", a=pa),
+                                in_=wb_scales[:, 4 * q : 4 * q + 4, :].bitcast(I32).rearrange("a r c -> r a c"))
+        nc.sync.dma_start(out=tab2_w[1][:], in_=words(tab2_words[1]))
+        nc.sync.dma_start(out=wc_raw[:], in_=wc_words.rearrange("a p c i -> p a (c i)").bitcast(I32))
+        nc.sync.dma_start(idx[:], offs)
+        nc.sync.dma_start(out=tab2_w[2][:], in_=words(tab2_words[2]))
+        nc.sync.dma_start(out=wb_raw[:], in_=wb_words.rearrange("a p c -> p a c").bitcast(I32))
+        nc.sync.dma_start(places[:], pos1)
+        nc.sync.dma_start(out=gain_sb[:], in_=gain.rearrange("(p t) -> p t", t=PACK))
+        nc.sync.dma_start(out=w3_raw[:], in_=w3.rearrange("(p j) c -> p j c", j=PACK))
+        for a in range(pa):
+            nc.sync.dma_start(out=wa_raw[:, PACK * H * a : PACK * H * (a + 1)],
+                              in_=wa[512 * a : 512 * (a + 1), :].rearrange("(p j) c -> p (j c)", j=PACK))
+        nc.sync.dma_start(out=tab_w[:].rearrange("p (a c) -> p a c", a=pa), in_=tab_words.rearrange("a p c i -> p a (c i)").bitcast(I32))
+        nc.sync.dma_start(out=w4_w[:], in_=w4_words[0].bitcast(I32))
+        load_planes(nc.sync, w4_sc, w4_scales, 1)
+
+        turned = bank("wgs_turned")
+        for e in range(NG // P):
+            nc.tensor.transpose(turned[:, P * e : P * (e + 1)], wgs_sb[:, P * e : P * (e + 1)], ident[:])
+        spread = [ring([P, PACK * P], F32, "spread%d" % e, "page%d" % e, 1) for e in range(NG // P)]
+        for e in range(NG // P):
+            src = turned[:, P * e : P * (e + 1)].rearrange("m (q t) -> m t q", t=PACK).unsqueeze(2).to_broadcast([P, PACK, 4, 32])
+            nc.scalar.copy(out=spread[e][:].rearrange("m (t g q) -> m t g q", t=PACK, g=4), in_=src)
+        wgs_rows = []
+        for t in range(PACK):
+            back = bank("wgs_back")
+            for e in range(NG // P):
+                nc.tensor.transpose(back[:, P * e : P * (e + 1)], spread[e][:, P * t : P * (t + 1)], ident[:])
+            dealt = held([P, NG], F32, "wgs_dealt%d" % t)
+            nc.scalar.copy(out=dealt[:], in_=back[:])
+            wgs_rows.append(dealt[:])
+
+        placed = [ring([P, S], F32, "placed%d" % t, "page%d" % t, 1) for t in range(PACK)]
+        for t in range(PACK):
+            nc.gpsimd.memset(placed[t][:], 0.0)
+
+        v2 = [held([P, NG], U32, "v2_%d" % a) for a in range(pb)]
+        v2_sc = held([P, NG], U8, "v2_sc")
+        v_sc0 = [held([P, HALF], U8, "v_sc0_0"), ring([P, HALF], U8, "v_sc0_1", "late", 1)]
+        nc.vector.tensor_copy(v2[0][:], tab2_w[0][:].bitcast(U32).indirect(idx2[:]))
+        nc.vector.tensor_copy(v2_sc[:], tab2_sc[:].indirect(idx2[:]))
+        nc.vector.tensor_copy(v2[1][:], tab2_w[1][:].bitcast(U32).indirect(idx2[:]))
+
+        wc_w = [held([P, H], I32, "wc_w%d" % a) for a in range(pb)]
+        for a in range(pb):
+            nc.vector.tensor_copy(out=wc_w[a][:].rearrange("p (t m) -> p m t", t=PACK),
+                                  in_=wc_raw[:, a, :].rearrange("p (m t) -> p m t", t=PACK))
+        wc_sc = held([P, H], U8, "wc_sc")
+        nc.vector.tensor_copy(out=wc_sc[:].rearrange("p (t m) -> p t m", t=PACK),
+                              in_=wc_sc_raw[:].rearrange("p (m t) -> p t m", t=PACK))
+        nc.vector.tensor_copy(v_sc0[0][:], tab_sc[:].indirect(idx[:, 0:32]))
+        nc.vector.tensor_copy(v2[2][:], tab2_w[2][:].bitcast(U32).indirect(idx2[:]))
+        nc.vector.tensor_copy(v_sc0[1][:], tab_sc[:].indirect(idx[:, 32:64]))
+        for h in range(2):
+            nc.gpsimd.dma_start(out=v_sc1[h][0:112, :].bitcast(I32), in_=v_sc0[h][4:116, :].bitcast(I32))
+
+        sig_all = ring([P, 2 * PACK * HALF], F32, "sig", "wa_sig", 1)
+        sig = [sig_all[:, PACK * HALF * h : PACK * HALF * (h + 1)].rearrange("p (t j) -> p t j", t=PACK) for h in range(2)]
+        b_sb = []
+
+        def gauge(t):
+            acc = bank("b_acc%d" % t)
+            cols = slice(P * t, P * (t + 1))
+            for a in range(pb):
+                nc.tensor.matmul_mx(out=acc[:], lhsT=wc_w[a][:, cols].bitcast(FP8X4), lhsT_scale=wc_sc[4 * a : P, cols],
+                                    rhs=v2[a][:].bitcast(FP8X4), rhs_scale=v2_sc[4 * a : P, :],
+                                    start=(a == 0), stop=(a == pb - 1))
+            b_t = held([P, NG], F32, "b%d" % t)
+            nc.scalar.activation(out=b_t[:], in_=acc[:], func=ACT.Copy, scale=gain_sb[:, t : t + 1])
+            b_sb.append(b_t)
+
+        for t in range(4):
+            gauge(t)
+        def interleaved(tile):
+            return tile.rearrange("p (c i t) -> p c t i", i=4, t=PACK)
+
+        def by_rows(view):
+            return view.rearrange("p t (c i) -> p c t i", i=4)
+
+        w3_bf = held([P, PACK * N], BF16, "w3_bf")
+        nc.scalar.copy(out=interleaved(w3_bf[:]), in_=by_rows(w3_raw[:]))
+        wa_w = [held([P, H], U32, "wa_w%d" % a) for a in range(pa)]
+        wa_sc = [held([P, H], U8, "wa_sc%d" % a) for a in range(pa)]
+        for a in range(pa):
+            wa_bf = held([P, PACK * H], BF16, "wa_bf%d" % a)
+            nc.scalar.copy(out=wa_bf[:].rearrange("p (t m j) -> p m j t", t=PACK, j=PACK),
+                           in_=wa_raw[:, PACK * H * a : PACK * H * (a + 1)].rearrange("p (j m t) -> p m j t", j=PACK, t=PACK))
+            nc.vector.quantize_mx(out=wa_w[a][:].bitcast(FP8X4), scales=wa_sc[a][:], in_=wa_bf[:])
+
+        def place(t):
+            nc.vector.tensor_tensor(placed[t][:].indirect(places[:]), b_sb[t][:], wgs_rows[t], ALU.mult)
+            for h in range(2):
+                nc.scalar.activation(out=sig[h][:, t, :], in_=placed[t][:, HALF * h : HALF * (h + 1)], func=ACT.Sigmoid)
+
+        for t in range(4):
+            place(t)
+
+        v = [[held([P, HALF], U32, "v%d_%d" % (a, h)) for h in range(2)] for a in range(pa)]
+
+        def gather_v(a, h):
+            nc.vector.tensor_copy(v[a][h][:], tab_w[:, T * a : T * (a + 1)].bitcast(U32).indirect(idx[:, 32 * h : 32 * (h + 1)]))
+
+        gather_v(0, 0)
+        wb_w = held([P, pa * H], U16, "wb_w")
+        nc.vector.tensor_copy(out=wb_w[:].rearrange("p (a t m) -> p a t m", a=pa, t=PACK),
+                              in_=wb_raw[:].rearrange("p a c -> p (a c)").bitcast(U16).rearrange("p (a m t) -> p a t m", a=pa, t=PACK))
+        v_sc = [[v_sc0[h][:] for h in range(2)], [v_sc1[h][:] for h in range(2)]]
+        wb_sc = held([P, pa * H], U8, "wb_sc")
+        nc.vector.tensor_copy(out=wb_sc[:].rearrange("p (a t m) -> p a t m", a=pa, t=PACK),
+                              in_=wb_sc_raw[:].rearrange("p (a m t) -> p a t m", a=pa, t=PACK))
+        gather_v(1, 0)
+        gather_v(0, 1)
+        gather_v(1, 1)
+
+        w3_w = ring([P, N], U32, "w3_w", "tab_w3", 1)
+        w3_sc = held([P, N], U8, "w3_sc")
+
+        a_f32 = [ring([P, PACK, HALF], F32, "a%d" % h, "a%d" % h, 1) for h in range(2)]
+        a_w, a_sc = [], []
+
+        def first_stage(h, tiles):
+            for t in tiles:
+                lin, dev = bank("lin"), bank("dev")
+                for a in range(pa):
+                    c0 = H * a + P * t
+                    nc.tensor.matmul_mx(out=dev[:], lhsT=wb_w[:, c0 : c0 + P].bitcast(FP4X4), lhsT_scale=wb_sc[:, c0 : c0 + P],
+                                        rhs=v[a][h][:].bitcast(FP8X4), rhs_scale=v_sc[a][h],
+                                        start=(a == 0), stop=(a == pa - 1))
+                for a in range(pa):
+                    cols = slice(P * t, P * (t + 1))
+                    nc.tensor.matmul_mx(out=lin[:], lhsT=wa_w[a][:, cols].bitcast(FP8X4), lhsT_scale=wa_sc[a][:, cols],
+                                        rhs=v[a][h][:].bitcast(FP8X4), rhs_scale=v_sc[a][h],
+                                        start=(a == 0), stop=(a == pa - 1))
+                sq = ring([P, HALF], F32, "sq", "sq", 4)
+                nc.scalar.activation(out=sq[:], in_=dev[:], func=ACT.Square)
+                nc.vector.tensor_tensor(out=a_f32[h][:, t, :], in0=lin[:], in1=sq[:], op=ALU.subtract)
+
+        def quantise_a(c):
+            h, c0 = divmod(c * CHUNK, HALF)
+            a_bf = ring([P, PACK * CHUNK], BF16, "a_bf", "a_bf", 2)
+            if c in [3]:
+                nc.vector.tensor_scalar(out=interleaved(a_bf[:]), in0=by_rows(a_f32[h][:, :, c0 : c0 + CHUNK]), scalar1=-1.0, scalar2=None, op0=ALU.mult)
+            else:
+                nc.scalar.activation(out=interleaved(a_bf[:]), in_=by_rows(a_f32[h][:, :, c0 : c0 + CHUNK]), func=ACT.Copy, scale=-1.0)
+            w = held([P, CHUNK], U32, "a_w%d" % c)
+            s = held([P, CHUNK], U8, "a_sc%d" % c)
+            nc.vector.quantize_mx(out=w[:].bitcast(FP8X4), scales=s[:], in_=a_bf[:])
+            a_w.append(w)
+            a_sc.append(s)
+
+        def second_stage(c):
+            h, c0 = divmod(c * CHUNK, HALF)
+            z_bf = ring([P, PACK * CHUNK], BF16, "z_bf", "z_bf", 2)
+            nc.vector.tensor_tensor(out=interleaved(z_bf[:]), in0=by_rows(a_f32[h][:, :, c0 : c0 + CHUNK]),
+                                    in1=by_rows(sig[h][:, :, c0 : c0 + CHUNK]), op=ALU.mult)
+            z_w = ring([P, CHUNK], U32, "z_w", "z_w", 2)
+            z_sc = ring([P, CHUNK], U8, "z_sc", "z_sc", 2)
+            nc.vector.quantize_mx(out=z_w[:].bitcast(FP8X4), scales=z_sc[:], in_=z_bf[:])
+            for pair in range(N // (2 * P)):
+                acc = bank("y")
+                for u in range(2):
+                    n0 = P * (2 * pair + u)
+                    for e in range(CHUNK // P):
+                        cols = slice(P * e, P * (e + 1))
+                        nc.tensor.matmul_mx(out=acc[:, CHUNK * u + P * e : CHUNK * u + P * (e + 1)],
+                                            lhsT=w4_w[:].bitcast(U8)[:, 2 * n0 : 2 * (n0 + P)].bitcast(FP4X4),
+                                            lhsT_scale=w4_sc[:, n0 : n0 + P],
+                                            rhs=a_w[c][:, cols].bitcast(FP8X4), rhs_scale=a_sc[c][:, cols],
+                                            start=(u == 0 and e == 0), stop=False)
+                for u in range(2):
+                    n0 = P * (2 * pair + u)
+                    nc.tensor.matmul_mx(out=acc[:, CHUNK * u : CHUNK * (u + 1)],
+                                        lhsT=w3_w[:, n0 : n0 + P].bitcast(FP8X4), lhsT_scale=w3_sc[:, n0 : n0 + P],
+                                        rhs=z_w[:].bitcast(FP8X4), rhs_scale=z_sc[:],
+                                        start=False, stop=(u == 1))
+                y = ring([P, 2, CHUNK], F32, "y_sb", "y_sb", 10)
+                flat = y[:].rearrange("p u j -> p (u j)")
+                if [c, pair] in [[3,1]]:
+                    nc.vector.tensor_copy(out=flat, in_=acc[:])
+                else:
+                    nc.scalar.copy(out=flat, in_=acc[:])
+                rows = out[2 * P * pair : 2 * P * (pair + 1), CHUNK * c : CHUNK * (c + 1)]
+                nc.sync.dma_start(out=rows.rearrange("(u p) j -> p u j", p=P), in_=y[:])
+
+        nc.vector.quantize_mx(out=w3_w[:, 0:512].bitcast(FP8X4), scales=w3_sc[:, 0:512], in_=w3_bf[:, 0:2048])
+        nc.vector.quantize_mx(out=w3_w[:, 512:N].bitcast(FP8X4), scales=w3_sc[:, 512:N], in_=w3_bf[:, 2048 : PACK * N])
+        first_stage(0, [0])
+        first_stage(0, [1])
+        first_stage(0, [2])
+        first_stage(0, [3])
+        quantise_a(0)
+        quantise_a(1)
+        first_stage(1, [0])
+        first_stage(1, [1])
+        first_stage(1, [2])
+        first_stage(1, [3])
+        second_stage(0)
+        quantise_a(2)
+        second_stage(1)
+        quantise_a(3)
+        second_stage(2)
+        second_stage(3)

@@ -3,8 +3,8 @@ from contextlib import ExitStack
 import concourse.mybir as mybir
 from concourse.masks import make_identity
 
-K, K2, T, T3, S, NG, H, N = 1024, 1536, 4096, 2048, 1024, 512, 512, 768
-FLOPS = 2 * (2 * K * H * S + K2 * H * NG + 2 * H * N * S)
+K, K2, T, T2, S, M, H, N = 1024, 1536, 4096, 2048, 1024, 512, 512, 768
+FLOPS = 2 * (2 * K * H * S + K2 * H * M + 2 * H * N * S)
 
 F32 = mybir.dt.float32
 BF16 = mybir.dt.bfloat16
@@ -19,8 +19,15 @@ ACT = mybir.ActivationFunctionType
 
 P = 128
 PACK = 4
+QUADS = 4
+PASSES = K // 512
+PASSES2 = K2 // 512
 HALF = 512
 CHUNK = 256
+CHUNKS = S // CHUNK
+SQUARE_BUFS = 4
+STEP_BUFS = 2
+STORE_BUFS = 8
 
 
 def tile_list_kick_warning_features_kernel(
@@ -28,7 +35,6 @@ def tile_list_kick_warning_features_kernel(
     wc_words, wc_scales, gain, wgs, w3, w4_words, w4_scales, out,
 ):
     nc = tc.nc
-    pa, pb = K // 512, K2 // 512
 
     with ExitStack() as ctx:
         lists = ctx.enter_context(tc.tile_pool(name="lists", bufs=1))
@@ -38,213 +44,220 @@ def tile_list_kick_warning_features_kernel(
         def held(shape, dtype, name):
             return keep.tile(shape, dtype, name=name, align_bytes=64)
 
-        def ring(shape, dtype, name, tag, bufs):
+        def shared(shape, dtype, name, tag, bufs=1):
             return keep.tile(shape, dtype, name=name, tag=tag, bufs=bufs, align_bytes=64)
 
         def bank(name):
             return psum.tile([P, 512], F32, name=name, tag="bank")
 
+        def quadrant(tile, q, rows):
+            return tile[32 * q : 32 * q + rows, :].bitcast(I32)
+
+        def interleaved(tile):
+            return tile.rearrange("p (c i t) -> p c t i", i=2, t=PACK)
+
+        def by_rows(view):
+            return view.rearrange("p t (c i) -> p c t i", i=2)
+
         idx = lists.tile([P, S // 16], U16, name="idx")
-        idx2 = lists.tile([P, NG // 16], U16, name="idx2")
-        places = lists.tile([P, NG // 16], U16, name="places")
+        idx2 = lists.tile([P, M // 16], U16, name="idx2")
+        places = lists.tile([P, M // 16], U16, name="places")
 
-        tab2_sc = held([P, T3], U8, "tab2_sc")
+        tab2_sc = held([P, T2], U8, "tab2_sc")
         tab_sc = held([P, T], U8, "tab_sc")
-        wc_sc_raw = held([P, H], U8, "wc_sc_raw")
-        wb_sc_raw = held([P, pa * H], U8, "wb_sc_raw")
+        wc_sc_raw = held([P, PASSES2 * H], U8, "wc_sc_raw")
+        wb_sc_raw = held([P, PASSES * H], U8, "wb_sc_raw")
         w4_sc = held([P, N], U8, "w4_sc")
-        v_sc1 = [held([P, HALF], U8, "v_sc1_%d" % h) for h in range(2)]
-        for tile in (tab2_sc, wc_sc_raw, tab_sc, wb_sc_raw, w4_sc, v_sc1[0], v_sc1[1]):
+        v_plane = [held([P, S], U8, "v_plane%d" % a) for a in range(PASSES)]
+        for tile in (tab_sc, tab2_sc, wc_sc_raw, wb_sc_raw):
             nc.vector.memset(tile[:].bitcast(I32), 0)
-
-        def words(dram):
-            return dram.rearrange("p c i -> p (c i)").bitcast(I32)
-
-        tab2_w = [ring([P, T3], I32, "tab2_w%d" % a, tag, 1) for a, tag in enumerate(("a0", "a1", "late"))]
-        tab_w = ring([P, pa * T], I32, "tab_w", "tab_w3", 1)
-        wc_raw = held([P, pb, H], I32, "wc_raw")
-        gain_sb = held([P, PACK], F32, "gain_sb")
-        wgs_sb = held([P, NG], F32, "wgs_sb")
         ident = held([P, P], F32, "ident")
         make_identity(nc, ident[:])
-        wb_raw = held([P, pa, H // 2], I32, "wb_raw")
-        wa_raw = ring([P, pa * PACK * H], F32, "wa_raw", "wa_sig", 1)
+        for tile in v_plane + [w4_sc]:
+            nc.gpsimd.memset(tile[:].bitcast(I32), 0)
+        page = [held([P, S], F32, "page%d" % t) for t in range(PACK)]
+        for t in range(PACK):
+            nc.gpsimd.memset(page[t][:], 0.0)
+
+        tab2_w = [shared([P, T2], I32, "tab2_w%d" % a, "tab2_then_a%d" % a) for a in range(PASSES2)]
+        tab_w = shared([P, PASSES * T], I32, "tab_w", "tab_then_w3")
+        wc_raw = held([P, PASSES2, H], I32, "wc_raw")
+        gain_sb = held([P, PACK], F32, "gain_sb")
+        wgs_sb = held([P, M], F32, "wgs_sb")
+        wb_raw = held([P, PASSES, H // 2], I32, "wb_raw")
+        wa_raw = shared([P, PASSES * PACK * H], F32, "wa_raw", "wa_then_sigmoid")
         w3_raw = held([P, PACK, N], F32, "w3_raw")
         w4_w = held([P, N // 2], I32, "w4_w")
 
-        def load_planes(queue, tile, scales, passes):
-            for q in range(4):
-                queue.dma_start(out=tile[32 * q : 32 * q + 4 * passes, :].bitcast(I32),
-                                in_=scales[:, 4 * q : 4 * q + 4, :].bitcast(I32))
+        def load_tab2(a):
+            nc.sync.dma_start(out=tab2_w[a][:], in_=tab2_words[a].rearrange("p c i -> p (c i)").bitcast(I32))
+
+        def load_planes_side_by_side(tile, scales, passes, quadrants):
+            for q in quadrants:
+                nc.sync.dma_start(out=quadrant(tile, q, 4).rearrange("s (a c) -> s a c", a=passes),
+                                  in_=scales[:, 4 * q : 4 * q + 4, :].bitcast(I32).rearrange("a s c -> s a c"))
 
         nc.sync.dma_start(idx2[:], offs2)
-        nc.sync.dma_start(out=tab2_w[0][:], in_=words(tab2_words[0]))
-        nc.scalar.dma_start(out=wgs_sb[:], in_=wgs)
-        load_planes(nc.gpsimd, tab2_sc, tab2_scales, pb)
-        load_planes(nc.scalar, wc_sc_raw, wc_scales, pb)
-        load_planes(nc.gpsimd, tab_sc, tab_scales, pa)
-        for q in range(4):
-            nc.scalar.dma_start(out=wb_sc_raw[32 * q : 32 * q + 4, :].bitcast(I32).rearrange("r (a c) -> r a c", a=pa),
-                                in_=wb_scales[:, 4 * q : 4 * q + 4, :].bitcast(I32).rearrange("a r c -> r a c"))
-        nc.sync.dma_start(out=tab2_w[1][:], in_=words(tab2_words[1]))
-        nc.sync.dma_start(out=wc_raw[:], in_=wc_words.rearrange("a p c i -> p a (c i)").bitcast(I32))
+        load_tab2(0)
+        nc.sync.dma_start(out=wgs_sb[:], in_=wgs)
         nc.sync.dma_start(idx[:], offs)
-        nc.sync.dma_start(out=tab2_w[2][:], in_=words(tab2_words[2]))
+        nc.sync.dma_start(out=tab_sc[0:P:4, :].bitcast(I32), in_=tab_scales.rearrange("a g c -> (a g) c").bitcast(I32))
+        load_tab2(1)
+        for q in range(QUADS):
+            nc.sync.dma_start(out=quadrant(tab2_sc, q, 4 * PASSES2), in_=tab2_scales[:, 4 * q : 4 * q + 4, :].bitcast(I32))
+        nc.sync.dma_start(out=wc_raw[:], in_=wc_words.rearrange("a p c i -> p a (c i)").bitcast(I32))
+        load_planes_side_by_side(wc_sc_raw, wc_scales, PASSES2, range(QUADS))
+        load_planes_side_by_side(wb_sc_raw, wb_scales, PASSES, range(QUADS // 2))
+        load_tab2(2)
+        load_planes_side_by_side(wb_sc_raw, wb_scales, PASSES, range(QUADS // 2, QUADS))
         nc.sync.dma_start(out=wb_raw[:], in_=wb_words.rearrange("a p c -> p a c").bitcast(I32))
         nc.sync.dma_start(places[:], pos1)
         nc.sync.dma_start(out=gain_sb[:], in_=gain.rearrange("(p t) -> p t", t=PACK))
-        nc.sync.dma_start(out=w3_raw[:], in_=w3.rearrange("(p j) c -> p j c", j=PACK))
-        for a in range(pa):
+        for a in range(PASSES):
             nc.sync.dma_start(out=wa_raw[:, PACK * H * a : PACK * H * (a + 1)],
                               in_=wa[512 * a : 512 * (a + 1), :].rearrange("(p j) c -> p (j c)", j=PACK))
-        nc.sync.dma_start(out=tab_w[:].rearrange("p (a c) -> p a c", a=pa), in_=tab_words.rearrange("a p c i -> p a (c i)").bitcast(I32))
-        nc.sync.dma_start(out=w4_w[:], in_=w4_words[0].bitcast(I32))
-        load_planes(nc.sync, w4_sc, w4_scales, 1)
+        nc.sync.dma_start(out=w3_raw[:], in_=w3.rearrange("(p j) c -> p j c", j=PACK))
 
         turned = bank("wgs_turned")
-        for e in range(NG // P):
+        for e in range(M // P):
             nc.tensor.transpose(turned[:, P * e : P * (e + 1)], wgs_sb[:, P * e : P * (e + 1)], ident[:])
-        spread = [ring([P, PACK * P], F32, "spread%d" % e, "page%d" % e, 1) for e in range(NG // P)]
-        for e in range(NG // P):
-            src = turned[:, P * e : P * (e + 1)].rearrange("m (q t) -> m t q", t=PACK).unsqueeze(2).to_broadcast([P, PACK, 4, 32])
-            nc.scalar.copy(out=spread[e][:].rearrange("m (t g q) -> m t g q", t=PACK, g=4), in_=src)
-        wgs_rows = []
+        spread = [held([P, PACK * P], F32, "spread%d" % e) for e in range(M // P)]
+        for e in range(M // P):
+            rows = turned[:, P * e : P * (e + 1)].rearrange("m (q t) -> m t q", t=PACK)
+            nc.scalar.copy(out=spread[e][:].rearrange("m (t g q) -> m t g q", t=PACK, g=QUADS),
+                           in_=rows.unsqueeze(2).to_broadcast([P, PACK, QUADS, 32]))
+        wgs_dealt = [held([P, M], F32, "wgs_dealt%d" % t) for t in range(PACK)]
         for t in range(PACK):
             back = bank("wgs_back")
-            for e in range(NG // P):
+            for e in range(M // P):
                 nc.tensor.transpose(back[:, P * e : P * (e + 1)], spread[e][:, P * t : P * (t + 1)], ident[:])
-            dealt = held([P, NG], F32, "wgs_dealt%d" % t)
-            nc.scalar.copy(out=dealt[:], in_=back[:])
-            wgs_rows.append(dealt[:])
+            nc.scalar.copy(out=wgs_dealt[t][:], in_=back[:])
 
-        placed = [ring([P, S], F32, "placed%d" % t, "page%d" % t, 1) for t in range(PACK)]
-        for t in range(PACK):
-            nc.gpsimd.memset(placed[t][:], 0.0)
+        v2 = [held([P, M], U32, "v2_%d" % a) for a in range(PASSES2)]
+        v2_sc = held([P, M], U8, "v2_sc")
+        v_sc_rows = held([P, S], U8, "v_sc_rows")
 
-        v2 = [held([P, NG], U32, "v2_%d" % a) for a in range(pb)]
-        v2_sc = held([P, NG], U8, "v2_sc")
-        v_sc0 = [held([P, HALF], U8, "v_sc0_0"), ring([P, HALF], U8, "v_sc0_1", "late", 1)]
-        nc.vector.tensor_copy(v2[0][:], tab2_w[0][:].bitcast(U32).indirect(idx2[:]))
+        def gather_v2(a):
+            nc.vector.tensor_copy(v2[a][:], tab2_w[a][:].bitcast(U32).indirect(idx2[:]))
+
+        gather_v2(0)
         nc.vector.tensor_copy(v2_sc[:], tab2_sc[:].indirect(idx2[:]))
-        nc.vector.tensor_copy(v2[1][:], tab2_w[1][:].bitcast(U32).indirect(idx2[:]))
+        gather_v2(1)
+        nc.vector.tensor_copy(v_sc_rows[:], tab_sc[:].indirect(idx[:]))
 
-        wc_w = [held([P, H], I32, "wc_w%d" % a) for a in range(pb)]
-        for a in range(pb):
+        def move_plane(a):
+            for q in range(QUADS):
+                first = 4 * (16 * a + 4 * q)
+                nc.sync.dma_start(out=quadrant(v_plane[a], q, 4), in_=v_sc_rows[first : first + 16 : 4, :].bitcast(I32))
+
+        move_plane(0)
+        nc.sync.dma_start(out=tab_w[:].rearrange("p (a c) -> p a c", a=PASSES),
+                          in_=tab_words.rearrange("a p c i -> p a (c i)").bitcast(I32))
+        move_plane(1)
+        nc.sync.dma_start(out=w4_w[:], in_=w4_words[0].bitcast(I32))
+        for q in range(QUADS):
+            nc.sync.dma_start(out=quadrant(w4_sc, q, 4), in_=w4_scales[0, 4 * q : 4 * q + 4, :].bitcast(I32))
+
+        def deal(dealt, raw, passes):
+            nc.vector.tensor_copy(out=dealt.rearrange("p (a t m) -> p a t m", a=passes, t=PACK),
+                                  in_=raw.rearrange("p (a m t) -> p a t m", a=passes, t=PACK))
+
+        wc_w = [held([P, H], I32, "wc_w%d" % a) for a in range(PASSES2)]
+        for a in range(PASSES2):
             nc.vector.tensor_copy(out=wc_w[a][:].rearrange("p (t m) -> p m t", t=PACK),
                                   in_=wc_raw[:, a, :].rearrange("p (m t) -> p m t", t=PACK))
-        wc_sc = held([P, H], U8, "wc_sc")
-        nc.vector.tensor_copy(out=wc_sc[:].rearrange("p (t m) -> p t m", t=PACK),
-                              in_=wc_sc_raw[:].rearrange("p (m t) -> p t m", t=PACK))
-        nc.vector.tensor_copy(v_sc0[0][:], tab_sc[:].indirect(idx[:, 0:32]))
-        nc.vector.tensor_copy(v2[2][:], tab2_w[2][:].bitcast(U32).indirect(idx2[:]))
-        nc.vector.tensor_copy(v_sc0[1][:], tab_sc[:].indirect(idx[:, 32:64]))
-        for h in range(2):
-            nc.gpsimd.dma_start(out=v_sc1[h][0:112, :].bitcast(I32), in_=v_sc0[h][4:116, :].bitcast(I32))
+        wc_sc = held([P, PASSES2 * H], U8, "wc_sc")
+        deal(wc_sc[:], wc_sc_raw[:], PASSES2)
+        gather_v2(2)
 
-        sig_all = ring([P, 2 * PACK * HALF], F32, "sig", "wa_sig", 1)
-        sig = [sig_all[:, PACK * HALF * h : PACK * HALF * (h + 1)].rearrange("p (t j) -> p t j", t=PACK) for h in range(2)]
-        b_sb = []
-
-        def gauge(t):
-            acc = bank("b_acc%d" % t)
-            cols = slice(P * t, P * (t + 1))
-            for a in range(pb):
-                nc.tensor.matmul_mx(out=acc[:], lhsT=wc_w[a][:, cols].bitcast(FP8X4), lhsT_scale=wc_sc[4 * a : P, cols],
+        sigmoid_all = shared([P, PACK * S], F32, "sigmoid", "wa_then_sigmoid")
+        sigmoid = [sigmoid_all[:, PACK * HALF * h : PACK * HALF * (h + 1)].rearrange("p (t j) -> p t j", t=PACK)
+                   for h in range(S // HALF)]
+        b = [held([P, M], F32, "b%d" % t) for t in range(PACK)]
+        for t in range(PACK):
+            acc = bank("b_acc")
+            order = list(range(PASSES2)) if t == 0 else list(reversed(range(PASSES2)))
+            for a in order:
+                nc.tensor.matmul_mx(out=acc[:], lhsT=wc_w[a][:, P * t : P * (t + 1)].bitcast(FP8X4),
+                                    lhsT_scale=wc_sc[:, H * a + P * t : H * a + P * (t + 1)],
                                     rhs=v2[a][:].bitcast(FP8X4), rhs_scale=v2_sc[4 * a : P, :],
-                                    start=(a == 0), stop=(a == pb - 1))
-            b_t = held([P, NG], F32, "b%d" % t)
-            nc.scalar.activation(out=b_t[:], in_=acc[:], func=ACT.Copy, scale=gain_sb[:, t : t + 1])
-            b_sb.append(b_t)
-
-        for t in range(4):
-            gauge(t)
-        def interleaved(tile):
-            return tile.rearrange("p (c i t) -> p c t i", i=4, t=PACK)
-
-        def by_rows(view):
-            return view.rearrange("p t (c i) -> p c t i", i=4)
+                                    start=(a == order[0]), stop=(a == order[-1]))
+            nc.scalar.activation(out=b[t][:], in_=acc[:], func=ACT.Copy, scale=gain_sb[:, t : t + 1])
 
         w3_bf = held([P, PACK * N], BF16, "w3_bf")
         nc.scalar.copy(out=interleaved(w3_bf[:]), in_=by_rows(w3_raw[:]))
-        wa_w = [held([P, H], U32, "wa_w%d" % a) for a in range(pa)]
-        wa_sc = [held([P, H], U8, "wa_sc%d" % a) for a in range(pa)]
-        for a in range(pa):
+        wa_w = [held([P, H], U32, "wa_w%d" % a) for a in range(PASSES)]
+        wa_sc = [held([P, H], U8, "wa_sc%d" % a) for a in range(PASSES)]
+        for a in range(PASSES):
             wa_bf = held([P, PACK * H], BF16, "wa_bf%d" % a)
-            nc.scalar.copy(out=wa_bf[:].rearrange("p (t m j) -> p m j t", t=PACK, j=PACK),
-                           in_=wa_raw[:, PACK * H * a : PACK * H * (a + 1)].rearrange("p (j m t) -> p m j t", j=PACK, t=PACK))
+            dealt = wa_bf[:].rearrange("p (t m j) -> p m j t", t=PACK, j=PACK)
+            raw = wa_raw[:, PACK * H * a : PACK * H * (a + 1)].rearrange("p (j m t) -> p m j t", j=PACK, t=PACK)
+            for t in range(0, PACK, 2):
+                nc.scalar.copy(out=dealt[:, :, :, t : t + 2], in_=raw[:, :, :, t : t + 2])
             nc.vector.quantize_mx(out=wa_w[a][:].bitcast(FP8X4), scales=wa_sc[a][:], in_=wa_bf[:])
 
-        def place(t):
-            nc.vector.tensor_tensor(placed[t][:].indirect(places[:]), b_sb[t][:], wgs_rows[t], ALU.mult)
-            for h in range(2):
-                nc.scalar.activation(out=sig[h][:, t, :], in_=placed[t][:, HALF * h : HALF * (h + 1)], func=ACT.Sigmoid)
+        for t in range(PACK):
+            nc.vector.tensor_tensor(page[t][:].indirect(places[:]), b[t][:], wgs_dealt[t][:], ALU.mult)
+            for h in range(S // HALF):
+                nc.scalar.activation(out=sigmoid[h][:, t, :], in_=page[t][:, HALF * h : HALF * (h + 1)], func=ACT.Sigmoid)
 
-        for t in range(4):
-            place(t)
+        wb_w = held([P, PASSES * H], U16, "wb_w")
+        deal(wb_w[:], wb_raw[:].rearrange("p a c -> p (a c)").bitcast(U16), PASSES)
+        wb_sc = held([P, PASSES * H], U8, "wb_sc")
+        deal(wb_sc[:], wb_sc_raw[:], PASSES)
+        v = [[held([P, HALF], U32, "v%d_%d" % (a, h)) for h in range(S // HALF)] for a in range(PASSES)]
+        for h in range(S // HALF):
+            entries = idx[:, HALF // 16 * h : HALF // 16 * (h + 1)]
+            for a in range(PASSES):
+                nc.vector.tensor_copy(v[a][h][:], tab_w[:, T * a : T * (a + 1)].bitcast(U32).indirect(entries))
 
-        v = [[held([P, HALF], U32, "v%d_%d" % (a, h)) for h in range(2)] for a in range(pa)]
-
-        def gather_v(a, h):
-            nc.vector.tensor_copy(v[a][h][:], tab_w[:, T * a : T * (a + 1)].bitcast(U32).indirect(idx[:, 32 * h : 32 * (h + 1)]))
-
-        gather_v(0, 0)
-        wb_w = held([P, pa * H], U16, "wb_w")
-        nc.vector.tensor_copy(out=wb_w[:].rearrange("p (a t m) -> p a t m", a=pa, t=PACK),
-                              in_=wb_raw[:].rearrange("p a c -> p (a c)").bitcast(U16).rearrange("p (a m t) -> p a t m", a=pa, t=PACK))
-        v_sc = [[v_sc0[h][:] for h in range(2)], [v_sc1[h][:] for h in range(2)]]
-        wb_sc = held([P, pa * H], U8, "wb_sc")
-        nc.vector.tensor_copy(out=wb_sc[:].rearrange("p (a t m) -> p a t m", a=pa, t=PACK),
-                              in_=wb_sc_raw[:].rearrange("p (a m t) -> p a t m", a=pa, t=PACK))
-        gather_v(1, 0)
-        gather_v(0, 1)
-        gather_v(1, 1)
-
-        w3_w = ring([P, N], U32, "w3_w", "tab_w3", 1)
+        w3_w = shared([P, N], U32, "w3_w", "tab_then_w3")
         w3_sc = held([P, N], U8, "w3_sc")
+        for c0, c1 in ((0, 512), (512, N)):
+            nc.vector.quantize_mx(out=w3_w[:, c0:c1].bitcast(FP8X4), scales=w3_sc[:, c0:c1], in_=w3_bf[:, PACK * c0 : PACK * c1])
 
-        a_f32 = [ring([P, PACK, HALF], F32, "a%d" % h, "a%d" % h, 1) for h in range(2)]
-        a_w, a_sc = [], []
+        a_f32 = [shared([P, PACK, HALF], F32, "a%d" % h, "tab2_then_a%d" % h) for h in range(S // HALF)]
+        neg_a_w = [held([P, CHUNK], U32, "neg_a_w%d" % c) for c in range(CHUNKS)]
+        neg_a_sc = [held([P, CHUNK], U8, "neg_a_sc%d" % c) for c in range(CHUNKS)]
 
-        def first_stage(h, tiles):
-            for t in tiles:
+        def first_stage(h):
+            for t in range(PACK):
                 lin, dev = bank("lin"), bank("dev")
-                for a in range(pa):
-                    c0 = H * a + P * t
-                    nc.tensor.matmul_mx(out=dev[:], lhsT=wb_w[:, c0 : c0 + P].bitcast(FP4X4), lhsT_scale=wb_sc[:, c0 : c0 + P],
-                                        rhs=v[a][h][:].bitcast(FP8X4), rhs_scale=v_sc[a][h],
-                                        start=(a == 0), stop=(a == pa - 1))
-                for a in range(pa):
+                for a in range(PASSES):
+                    cols = slice(H * a + P * t, H * a + P * (t + 1))
+                    nc.tensor.matmul_mx(out=dev[:], lhsT=wb_w[:, cols].bitcast(FP4X4), lhsT_scale=wb_sc[:, cols],
+                                        rhs=v[a][h][:].bitcast(FP8X4), rhs_scale=v_plane[a][:, HALF * h : HALF * (h + 1)],
+                                        start=(a == 0), stop=(a == PASSES - 1))
+                for a in range(PASSES):
                     cols = slice(P * t, P * (t + 1))
                     nc.tensor.matmul_mx(out=lin[:], lhsT=wa_w[a][:, cols].bitcast(FP8X4), lhsT_scale=wa_sc[a][:, cols],
-                                        rhs=v[a][h][:].bitcast(FP8X4), rhs_scale=v_sc[a][h],
-                                        start=(a == 0), stop=(a == pa - 1))
-                sq = ring([P, HALF], F32, "sq", "sq", 4)
-                nc.scalar.activation(out=sq[:], in_=dev[:], func=ACT.Square)
-                nc.vector.tensor_tensor(out=a_f32[h][:, t, :], in0=lin[:], in1=sq[:], op=ALU.subtract)
+                                        rhs=v[a][h][:].bitcast(FP8X4), rhs_scale=v_plane[a][:, HALF * h : HALF * (h + 1)],
+                                        start=(a == 0), stop=(a == PASSES - 1))
+                square = shared([P, HALF], F32, "square", "square", SQUARE_BUFS)
+                nc.scalar.activation(out=square[:], in_=dev[:], func=ACT.Square)
+                nc.vector.tensor_tensor(out=a_f32[h][:, t, :], in0=lin[:], in1=square[:], op=ALU.subtract)
 
-        def quantise_a(c):
-            h, c0 = divmod(c * CHUNK, HALF)
-            a_bf = ring([P, PACK * CHUNK], BF16, "a_bf", "a_bf", 2)
-            if c in [3]:
-                nc.vector.tensor_scalar(out=interleaved(a_bf[:]), in0=by_rows(a_f32[h][:, :, c0 : c0 + CHUNK]), scalar1=-1.0, scalar2=None, op0=ALU.mult)
+        def chunk_of(halves, c):
+            h, j0 = divmod(c * CHUNK, HALF)
+            return by_rows(halves[h][:, :, j0 : j0 + CHUNK])
+
+        def quantise_neg_a(c):
+            neg_a_bf = shared([P, PACK * CHUNK], BF16, "neg_a_bf", "neg_a_bf", STEP_BUFS)
+            if c == CHUNKS - 1:
+                nc.vector.tensor_scalar(out=interleaved(neg_a_bf[:]), in0=chunk_of(a_f32, c), scalar1=-1.0, scalar2=None,
+                                        op0=ALU.mult)
             else:
-                nc.scalar.activation(out=interleaved(a_bf[:]), in_=by_rows(a_f32[h][:, :, c0 : c0 + CHUNK]), func=ACT.Copy, scale=-1.0)
-            w = held([P, CHUNK], U32, "a_w%d" % c)
-            s = held([P, CHUNK], U8, "a_sc%d" % c)
-            nc.vector.quantize_mx(out=w[:].bitcast(FP8X4), scales=s[:], in_=a_bf[:])
-            a_w.append(w)
-            a_sc.append(s)
+                nc.scalar.activation(out=interleaved(neg_a_bf[:]), in_=chunk_of(a_f32, c), func=ACT.Copy, scale=-1.0)
+            nc.vector.quantize_mx(out=neg_a_w[c][:].bitcast(FP8X4), scales=neg_a_sc[c][:], in_=neg_a_bf[:])
 
-        def second_stage(c):
-            h, c0 = divmod(c * CHUNK, HALF)
-            z_bf = ring([P, PACK * CHUNK], BF16, "z_bf", "z_bf", 2)
-            nc.vector.tensor_tensor(out=interleaved(z_bf[:]), in0=by_rows(a_f32[h][:, :, c0 : c0 + CHUNK]),
-                                    in1=by_rows(sig[h][:, :, c0 : c0 + CHUNK]), op=ALU.mult)
-            z_w = ring([P, CHUNK], U32, "z_w", "z_w", 2)
-            z_sc = ring([P, CHUNK], U8, "z_sc", "z_sc", 2)
+        def last_stage(c):
+            z_bf = shared([P, PACK * CHUNK], BF16, "z_bf", "z_bf", STEP_BUFS)
+            nc.vector.tensor_tensor(out=interleaved(z_bf[:]), in0=chunk_of(a_f32, c), in1=chunk_of(sigmoid, c), op=ALU.mult)
+            z_w = shared([P, CHUNK], U32, "z_w", "z_w", STEP_BUFS)
+            z_sc = shared([P, CHUNK], U8, "z_sc", "z_sc", STEP_BUFS)
             nc.vector.quantize_mx(out=z_w[:].bitcast(FP8X4), scales=z_sc[:], in_=z_bf[:])
             for pair in range(N // (2 * P)):
-                acc = bank("y")
+                acc = bank("y_acc")
                 for u in range(2):
                     n0 = P * (2 * pair + u)
                     for e in range(CHUNK // P):
@@ -252,7 +265,7 @@ def tile_list_kick_warning_features_kernel(
                         nc.tensor.matmul_mx(out=acc[:, CHUNK * u + P * e : CHUNK * u + P * (e + 1)],
                                             lhsT=w4_w[:].bitcast(U8)[:, 2 * n0 : 2 * (n0 + P)].bitcast(FP4X4),
                                             lhsT_scale=w4_sc[:, n0 : n0 + P],
-                                            rhs=a_w[c][:, cols].bitcast(FP8X4), rhs_scale=a_sc[c][:, cols],
+                                            rhs=neg_a_w[c][:, cols].bitcast(FP8X4), rhs_scale=neg_a_sc[c][:, cols],
                                             start=(u == 0 and e == 0), stop=False)
                 for u in range(2):
                     n0 = P * (2 * pair + u)
@@ -260,30 +273,20 @@ def tile_list_kick_warning_features_kernel(
                                         lhsT=w3_w[:, n0 : n0 + P].bitcast(FP8X4), lhsT_scale=w3_sc[:, n0 : n0 + P],
                                         rhs=z_w[:].bitcast(FP8X4), rhs_scale=z_sc[:],
                                         start=False, stop=(u == 1))
-                y = ring([P, 2, CHUNK], F32, "y_sb", "y_sb", 10)
+                y = shared([P, 2, CHUNK], F32, "y", "y", STORE_BUFS)
                 flat = y[:].rearrange("p u j -> p (u j)")
-                if [c, pair] in [[3,1]]:
+                if c == CHUNKS - 1 and pair == 1:
                     nc.vector.tensor_copy(out=flat, in_=acc[:])
                 else:
                     nc.scalar.copy(out=flat, in_=acc[:])
                 rows = out[2 * P * pair : 2 * P * (pair + 1), CHUNK * c : CHUNK * (c + 1)]
                 nc.sync.dma_start(out=rows.rearrange("(u p) j -> p u j", p=P), in_=y[:])
 
-        nc.vector.quantize_mx(out=w3_w[:, 0:512].bitcast(FP8X4), scales=w3_sc[:, 0:512], in_=w3_bf[:, 0:2048])
-        nc.vector.quantize_mx(out=w3_w[:, 512:N].bitcast(FP8X4), scales=w3_sc[:, 512:N], in_=w3_bf[:, 2048 : PACK * N])
-        first_stage(0, [0])
-        first_stage(0, [1])
-        first_stage(0, [2])
-        first_stage(0, [3])
-        quantise_a(0)
-        quantise_a(1)
-        first_stage(1, [0])
-        first_stage(1, [1])
-        first_stage(1, [2])
-        first_stage(1, [3])
-        second_stage(0)
-        quantise_a(2)
-        second_stage(1)
-        quantise_a(3)
-        second_stage(2)
-        second_stage(3)
+        first_stage(0)
+        quantise_neg_a(0)
+        quantise_neg_a(1)
+        first_stage(1)
+        for c in range(CHUNKS):
+            last_stage(c)
+            if c + 2 < CHUNKS:
+                quantise_neg_a(c + 2)

from contextlib import ExitStack

import concourse.mybir as mybir
from concourse.masks import make_identity

K, K2, T, T2, S, M, H, N = 1024, 1536, 4096, 2048, 1024, 512, 512, 768
FLOPS = 2 * (2 * K * H * S + K2 * H * M + 2 * H * N * S)

F32 = mybir.dt.float32
BF16 = mybir.dt.bfloat16
I32 = mybir.dt.int32
U32 = mybir.dt.uint32
U16 = mybir.dt.uint16
U8 = mybir.dt.uint8
FP8X4 = mybir.dt.float8_e4m3fn_x4
FP4X4 = mybir.dt.float4_e2m1fn_x4
ALU = mybir.AluOpType
ACT = mybir.ActivationFunctionType

P = 128
PACK = 4
QUADS = 4
PASSES = K // 512
PASSES2 = K2 // 512
HALF = 512
CHUNK = 256
CHUNKS = S // CHUNK
SQUARE_BUFS = 4
STEP_BUFS = 2
STORE_BUFS = 8


def tile_list_kick_warning_features_kernel(
    tc, tab_words, tab_scales, tab2_words, tab2_scales, offs, offs2, pos1, wa, wb_words, wb_scales,
    wc_words, wc_scales, gain, wgs, w3, w4_words, w4_scales, out,
):
    nc = tc.nc

    with ExitStack() as ctx:
        lists = ctx.enter_context(tc.tile_pool(name="lists", bufs=1))
        keep = ctx.enter_context(tc.tile_pool(name="keep", bufs=1))
        psum = ctx.enter_context(tc.psum_pool(name="psum", bufs=8))

        def held(shape, dtype, name):
            return keep.tile(shape, dtype, name=name, align_bytes=64)

        def shared(shape, dtype, name, tag, bufs=1):
            return keep.tile(shape, dtype, name=name, tag=tag, bufs=bufs, align_bytes=64)

        def bank(name):
            return psum.tile([P, 512], F32, name=name, tag="bank")

        def quadrant(tile, q, rows):
            return tile[32 * q : 32 * q + rows, :].bitcast(I32)

        def interleaved(tile):
            return tile.rearrange("p (c i t) -> p c t i", i=2, t=PACK)

        def by_rows(view):
            return view.rearrange("p t (c i) -> p c t i", i=2)

        idx = lists.tile([P, S // 16], U16, name="idx")
        idx2 = lists.tile([P, M // 16], U16, name="idx2")
        places = lists.tile([P, M // 16], U16, name="places")

        tab2_sc = held([P, T2], U8, "tab2_sc")
        tab_sc = held([P, T], U8, "tab_sc")
        wc_sc_raw = held([P, PASSES2 * H], U8, "wc_sc_raw")
        wb_sc_raw = held([P, PASSES * H], U8, "wb_sc_raw")
        w4_sc = held([P, N], U8, "w4_sc")
        v_plane = [held([P, S], U8, "v_plane%d" % a) for a in range(PASSES)]
        for tile in (tab_sc, tab2_sc, wc_sc_raw, wb_sc_raw):
            nc.vector.memset(tile[:].bitcast(I32), 0)
        ident = held([P, P], F32, "ident")
        make_identity(nc, ident[:])
        for tile in v_plane + [w4_sc]:
            nc.gpsimd.memset(tile[:].bitcast(I32), 0)
        page = [held([P, S], F32, "page%d" % t) for t in range(PACK)]
        for t in range(PACK):
            nc.gpsimd.memset(page[t][:], 0.0)

        tab2_w = [shared([P, T2], I32, "tab2_w%d" % a, "tab2_then_a%d" % a) for a in range(PASSES2)]
        tab_w = shared([P, PASSES * T], I32, "tab_w", "tab_then_w3")
        wc_raw = held([P, PASSES2, H], I32, "wc_raw")
        gain_sb = held([P, PACK], F32, "gain_sb")
        wgs_sb = held([P, M], F32, "wgs_sb")
        wb_raw = held([P, PASSES, H // 2], I32, "wb_raw")
        wa_raw = shared([P, PASSES * PACK * H], F32, "wa_raw", "wa_then_sigmoid")
        w3_raw = held([P, PACK, N], F32, "w3_raw")
        w4_w = held([P, N // 2], I32, "w4_w")

        def load_tab2(a):
            nc.sync.dma_start(out=tab2_w[a][:], in_=tab2_words[a].rearrange("p c i -> p (c i)").bitcast(I32))

        def load_planes_side_by_side(tile, scales, passes, quadrants):
            for q in quadrants:
                nc.sync.dma_start(out=quadrant(tile, q, 4).rearrange("s (a c) -> s a c", a=passes),
                                  in_=scales[:, 4 * q : 4 * q + 4, :].bitcast(I32).rearrange("a s c -> s a c"))

        nc.sync.dma_start(idx2[:], offs2)
        load_tab2(0)
        nc.sync.dma_start(out=wgs_sb[:], in_=wgs)
        nc.sync.dma_start(idx[:], offs)
        nc.sync.dma_start(out=tab_sc[0:P:4, :].bitcast(I32), in_=tab_scales.rearrange("a g c -> (a g) c").bitcast(I32))
        load_tab2(1)
        for q in range(QUADS):
            nc.sync.dma_start(out=quadrant(tab2_sc, q, 4 * PASSES2), in_=tab2_scales[:, 4 * q : 4 * q + 4, :].bitcast(I32))
        nc.sync.dma_start(out=wc_raw[:], in_=wc_words.rearrange("a p c i -> p a (c i)").bitcast(I32))
        load_planes_side_by_side(wc_sc_raw, wc_scales, PASSES2, range(QUADS))
        load_planes_side_by_side(wb_sc_raw, wb_scales, PASSES, range(QUADS // 2))
        load_tab2(2)
        load_planes_side_by_side(wb_sc_raw, wb_scales, PASSES, range(QUADS // 2, QUADS))
        nc.sync.dma_start(out=wb_raw[:], in_=wb_words.rearrange("a p c -> p a c").bitcast(I32))
        nc.sync.dma_start(places[:], pos1)
        nc.sync.dma_start(out=gain_sb[:], in_=gain.rearrange("(p t) -> p t", t=PACK))
        for a in range(PASSES):
            nc.sync.dma_start(out=wa_raw[:, PACK * H * a : PACK * H * (a + 1)],
                              in_=wa[512 * a : 512 * (a + 1), :].rearrange("(p j) c -> p (j c)", j=PACK))
        nc.sync.dma_start(out=w3_raw[:], in_=w3.rearrange("(p j) c -> p j c", j=PACK))

        turned = bank("wgs_turned")
        for e in range(M // P):
            nc.tensor.transpose(turned[:, P * e : P * (e + 1)], wgs_sb[:, P * e : P * (e + 1)], ident[:])
        spread = [held([P, PACK * P], F32, "spread%d" % e) for e in range(M // P)]
        for e in range(M // P):
            rows = turned[:, P * e : P * (e + 1)].rearrange("m (q t) -> m t q", t=PACK)
            nc.scalar.copy(out=spread[e][:].rearrange("m (t g q) -> m t g q", t=PACK, g=QUADS),
                           in_=rows.unsqueeze(2).to_broadcast([P, PACK, QUADS, 32]))
        wgs_dealt = [held([P, M], F32, "wgs_dealt%d" % t) for t in range(PACK)]
        for t in range(PACK):
            back = bank("wgs_back")
            for e in range(M // P):
                nc.tensor.transpose(back[:, P * e : P * (e + 1)], spread[e][:, P * t : P * (t + 1)], ident[:])
            nc.scalar.copy(out=wgs_dealt[t][:], in_=back[:])

        v2 = [held([P, M], U32, "v2_%d" % a) for a in range(PASSES2)]
        v2_sc = held([P, M], U8, "v2_sc")
        v_sc_rows = held([P, S], U8, "v_sc_rows")

        def gather_v2(a):
            nc.vector.tensor_copy(v2[a][:], tab2_w[a][:].bitcast(U32).indirect(idx2[:]))

        gather_v2(0)
        nc.vector.tensor_copy(v2_sc[:], tab2_sc[:].indirect(idx2[:]))
        gather_v2(1)
        nc.vector.tensor_copy(v_sc_rows[:], tab_sc[:].indirect(idx[:]))

        def move_plane(a):
            for q in range(QUADS):
                first = 4 * (16 * a + 4 * q)
                nc.sync.dma_start(out=quadrant(v_plane[a], q, 4), in_=v_sc_rows[first : first + 16 : 4, :].bitcast(I32))

        move_plane(0)
        nc.sync.dma_start(out=tab_w[:].rearrange("p (a c) -> p a c", a=PASSES),
                          in_=tab_words.rearrange("a p c i -> p a (c i)").bitcast(I32))
        move_plane(1)
        nc.sync.dma_start(out=w4_w[:], in_=w4_words[0].bitcast(I32))
        for q in range(QUADS):
            nc.sync.dma_start(out=quadrant(w4_sc, q, 4), in_=w4_scales[0, 4 * q : 4 * q + 4, :].bitcast(I32))

        def deal(dealt, raw, passes):
            nc.vector.tensor_copy(out=dealt.rearrange("p (a t m) -> p a t m", a=passes, t=PACK),
                                  in_=raw.rearrange("p (a m t) -> p a t m", a=passes, t=PACK))

        wc_w = [held([P, H], I32, "wc_w%d" % a) for a in range(PASSES2)]
        for a in range(PASSES2):
            nc.vector.tensor_copy(out=wc_w[a][:].rearrange("p (t m) -> p m t", t=PACK),
                                  in_=wc_raw[:, a, :].rearrange("p (m t) -> p m t", t=PACK))
        wc_sc = held([P, PASSES2 * H], U8, "wc_sc")
        deal(wc_sc[:], wc_sc_raw[:], PASSES2)
        gather_v2(2)

        sigmoid_all = shared([P, PACK * S], F32, "sigmoid", "wa_then_sigmoid")
        sigmoid = [sigmoid_all[:, PACK * HALF * h : PACK * HALF * (h + 1)].rearrange("p (t j) -> p t j", t=PACK)
                   for h in range(S // HALF)]
        b = [held([P, M], F32, "b%d" % t) for t in range(PACK)]
        for t in range(PACK):
            acc = bank("b_acc")
            order = list(range(PASSES2)) if t == 0 else list(reversed(range(PASSES2)))
            for a in order:
                nc.tensor.matmul_mx(out=acc[:], lhsT=wc_w[a][:, P * t : P * (t + 1)].bitcast(FP8X4),
                                    lhsT_scale=wc_sc[:, H * a + P * t : H * a + P * (t + 1)],
                                    rhs=v2[a][:].bitcast(FP8X4), rhs_scale=v2_sc[4 * a : P, :],
                                    start=(a == order[0]), stop=(a == order[-1]))
            nc.scalar.activation(out=b[t][:], in_=acc[:], func=ACT.Copy, scale=gain_sb[:, t : t + 1])

        w3_bf = held([P, PACK * N], BF16, "w3_bf")
        nc.scalar.copy(out=interleaved(w3_bf[:]), in_=by_rows(w3_raw[:]))
        wa_w = [held([P, H], U32, "wa_w%d" % a) for a in range(PASSES)]
        wa_sc = [held([P, H], U8, "wa_sc%d" % a) for a in range(PASSES)]
        for a in range(PASSES):
            wa_bf = held([P, PACK * H], BF16, "wa_bf%d" % a)
            dealt = wa_bf[:].rearrange("p (t m j) -> p m j t", t=PACK, j=PACK)
            raw = wa_raw[:, PACK * H * a : PACK * H * (a + 1)].rearrange("p (j m t) -> p m j t", j=PACK, t=PACK)
            for t in range(0, PACK, 2):
                nc.scalar.copy(out=dealt[:, :, :, t : t + 2], in_=raw[:, :, :, t : t + 2])
            nc.vector.quantize_mx(out=wa_w[a][:].bitcast(FP8X4), scales=wa_sc[a][:], in_=wa_bf[:])

        for t in range(PACK):
            nc.vector.tensor_tensor(page[t][:].indirect(places[:]), b[t][:], wgs_dealt[t][:], ALU.mult)
            for h in range(S // HALF):
                nc.scalar.activation(out=sigmoid[h][:, t, :], in_=page[t][:, HALF * h : HALF * (h + 1)], func=ACT.Sigmoid)

        wb_w = held([P, PASSES * H], U16, "wb_w")
        deal(wb_w[:], wb_raw[:].rearrange("p a c -> p (a c)").bitcast(U16), PASSES)
        wb_sc = held([P, PASSES * H], U8, "wb_sc")
        deal(wb_sc[:], wb_sc_raw[:], PASSES)
        v = [[held([P, HALF], U32, "v%d_%d" % (a, h)) for h in range(S // HALF)] for a in range(PASSES)]
        for h in range(S // HALF):
            entries = idx[:, HALF // 16 * h : HALF // 16 * (h + 1)]
            for a in range(PASSES):
                nc.vector.tensor_copy(v[a][h][:], tab_w[:, T * a : T * (a + 1)].bitcast(U32).indirect(entries))

        w3_w = shared([P, N], U32, "w3_w", "tab_then_w3")
        w3_sc = held([P, N], U8, "w3_sc")
        for c0, c1 in ((0, 512), (512, N)):
            nc.vector.quantize_mx(out=w3_w[:, c0:c1].bitcast(FP8X4), scales=w3_sc[:, c0:c1], in_=w3_bf[:, PACK * c0 : PACK * c1])

        a_f32 = [shared([P, PACK, HALF], F32, "a%d" % h, "tab2_then_a%d" % h) for h in range(S // HALF)]
        neg_a_w = [held([P, CHUNK], U32, "neg_a_w%d" % c) for c in range(CHUNKS)]
        neg_a_sc = [held([P, CHUNK], U8, "neg_a_sc%d" % c) for c in range(CHUNKS)]

        def first_stage(h):
            for t in range(PACK):
                lin, dev = bank("lin"), bank("dev")
                for a in range(PASSES):
                    cols = slice(H * a + P * t, H * a + P * (t + 1))
                    nc.tensor.matmul_mx(out=dev[:], lhsT=wb_w[:, cols].bitcast(FP4X4), lhsT_scale=wb_sc[:, cols],
                                        rhs=v[a][h][:].bitcast(FP8X4), rhs_scale=v_plane[a][:, HALF * h : HALF * (h + 1)],
                                        start=(a == 0), stop=(a == PASSES - 1))
                for a in range(PASSES):
                    cols = slice(P * t, P * (t + 1))
                    nc.tensor.matmul_mx(out=lin[:], lhsT=wa_w[a][:, cols].bitcast(FP8X4), lhsT_scale=wa_sc[a][:, cols],
                                        rhs=v[a][h][:].bitcast(FP8X4), rhs_scale=v_plane[a][:, HALF * h : HALF * (h + 1)],
                                        start=(a == 0), stop=(a == PASSES - 1))
                square = shared([P, HALF], F32, "square", "square", SQUARE_BUFS)
                nc.scalar.activation(out=square[:], in_=dev[:], func=ACT.Square)
                nc.vector.tensor_tensor(out=a_f32[h][:, t, :], in0=lin[:], in1=square[:], op=ALU.subtract)

        def chunk_of(halves, c):
            h, j0 = divmod(c * CHUNK, HALF)
            return by_rows(halves[h][:, :, j0 : j0 + CHUNK])

        def quantise_neg_a(c):
            neg_a_bf = shared([P, PACK * CHUNK], BF16, "neg_a_bf", "neg_a_bf", STEP_BUFS)
            if c == CHUNKS - 1:
                nc.vector.tensor_scalar(out=interleaved(neg_a_bf[:]), in0=chunk_of(a_f32, c), scalar1=-1.0, scalar2=None,
                                        op0=ALU.mult)
            else:
                nc.scalar.activation(out=interleaved(neg_a_bf[:]), in_=chunk_of(a_f32, c), func=ACT.Copy, scale=-1.0)
            nc.vector.quantize_mx(out=neg_a_w[c][:].bitcast(FP8X4), scales=neg_a_sc[c][:], in_=neg_a_bf[:])

        def last_stage(c):
            z_bf = shared([P, PACK * CHUNK], BF16, "z_bf", "z_bf", STEP_BUFS)
            nc.vector.tensor_tensor(out=interleaved(z_bf[:]), in0=chunk_of(a_f32, c), in1=chunk_of(sigmoid, c), op=ALU.mult)
            z_w = shared([P, CHUNK], U32, "z_w", "z_w", STEP_BUFS)
            z_sc = shared([P, CHUNK], U8, "z_sc", "z_sc", STEP_BUFS)
            nc.vector.quantize_mx(out=z_w[:].bitcast(FP8X4), scales=z_sc[:], in_=z_bf[:])
            for pair in range(N // (2 * P)):
                acc = bank("y_acc")
                for u in range(2):
                    n0 = P * (2 * pair + u)
                    for e in range(CHUNK // P):
                        cols = slice(P * e, P * (e + 1))
                        nc.tensor.matmul_mx(out=acc[:, CHUNK * u + P * e : CHUNK * u + P * (e + 1)],
                                            lhsT=w4_w[:].bitcast(U8)[:, 2 * n0 : 2 * (n0 + P)].bitcast(FP4X4),
                                            lhsT_scale=w4_sc[:, n0 : n0 + P],
                                            rhs=neg_a_w[c][:, cols].bitcast(FP8X4), rhs_scale=neg_a_sc[c][:, cols],
                                            start=(u == 0 and e == 0), stop=False)
                for u in range(2):
                    n0 = P * (2 * pair + u)
                    nc.tensor.matmul_mx(out=acc[:, CHUNK * u : CHUNK * (u + 1)],
                                        lhsT=w3_w[:, n0 : n0 + P].bitcast(FP8X4), lhsT_scale=w3_sc[:, n0 : n0 + P],
                                        rhs=z_w[:].bitcast(FP8X4), rhs_scale=z_sc[:],
                                        start=False, stop=(u == 1))
                y = shared([P, 2, CHUNK], F32, "y", "y", STORE_BUFS)
                flat = y[:].rearrange("p u j -> p (u j)")
                if c == CHUNKS - 1 and pair == 1:
                    nc.vector.tensor_copy(out=flat, in_=acc[:])
                else:
                    nc.scalar.copy(out=flat, in_=acc[:])
                rows = out[2 * P * pair : 2 * P * (pair + 1), CHUNK * c : CHUNK * (c + 1)]
                nc.sync.dma_start(out=rows.rearrange("(u p) j -> p u j", p=P), in_=y[:])

        first_stage(0)
        quantise_neg_a(0)
        quantise_neg_a(1)
        first_stage(1)
        for c in range(CHUNKS):
            last_stage(c)
            if c + 2 < CHUNKS:
                quantise_neg_a(c + 2)
